import numpy as np, ml_dtypes
CORES = [36,164,52,180,100,228,116,244]
N = 8
import mx_ref
BF = ml_dtypes.bfloat16
def gentries(a):
    return np.ascontiguousarray(a.reshape(8, 16, -1).transpose(0, 2, 1)).reshape(8, -1)
def gtable(e):
    e = np.asarray(e); return np.ascontiguousarray(e.reshape(8, -1, 16).transpose(0, 2, 1)).reshape(128, -1).astype(np.int32)
def gcols(t, e):
    v = np.concatenate([t.reshape(8, 16, -1, 4), np.zeros((8, 16, 1, 4), BF)], axis=2)
    return np.ascontiguousarray(np.stack([v[g][:, e[g]] for g in range(8)])).reshape(128, -1)
def gpick(z, e):
    return np.concatenate([z[16 * g:16 * g + 16][:, e[g]] for g in range(8)])
def tile(rs):
    return np.stack(rs, axis=2).reshape(128, -1).astype(BF)
def pick(q, e):
    c = np.concatenate([q[0].reshape(128, -1, 4), np.zeros((128, 1, 4), np.uint8)], axis=1); s = np.concatenate([q[1], np.ones((16, 1), np.uint8)], axis=1)
    return (np.ascontiguousarray(c[:, e].reshape(128, -1)), np.ascontiguousarray(s[:, e]))
def join(*qs):
    return (np.concatenate([q[0] for q in qs], axis=1), np.concatenate([q[1] for q in qs], axis=1))
def put(q, e, v):
    c, s = q[0].reshape(128, -1, 4).copy(), q[1].copy(); c[:, e] = v[0].reshape(128, -1, 4); s[:, e] = v[1]
    return (c.reshape(128, -1), s)
def pk(c, s):
    return (np.ascontiguousarray(c), mx_ref.live(s))
def emit(q):
    return q[0], q[1]
def packed(v, rng):
    q = [mx_ref.quantize(np.ascontiguousarray(v[r])) for r in range(N)]
    return np.stack([a for a, b in q]), np.stack([mx_ref.plane(b, rng) for a, b in q])
def values_of_codes():
    e, c = np.zeros((128, 128, 4), np.float32), np.zeros((128, 2, 4), np.uint8)
    e[np.arange(128), np.arange(128), 0] = 1
    c[:127, :, 0] = np.arange(256).reshape(2, 128).T[:127]
    return mx_ref.matmul(mx_ref.quantize(e.reshape(128, 512).astype(BF)), (c.reshape(128, 8), np.full((16, 2), 127, np.uint8))).T.reshape(-1).astype(np.float64)
CODE_VALUE, SCALE_VALUE = values_of_codes(), 2.0 ** (np.arange(256) - 127.0)
def decode(q):
    return (CODE_VALUE[q[0]].reshape(16, 8, -1, 4) * SCALE_VALUE[q[1]][:, None, :, None] + 0.0).reshape(128, -1).astype(np.float32)
def f(rng, *shape):
    return mx_ref.flush((rng.standard_normal(shape, dtype=np.float32) * np.exp2(rng.integers(-2, 3, shape[:-1] + (1,)))).astype(BF))
def wide(rng, *shape, cols=0):
    v = rng.standard_normal(shape, dtype=np.float32) * np.exp2(rng.integers(-12, 13, shape)).astype(np.float32)
    if cols: v *= np.repeat(np.exp2(rng.integers(-cols, cols + 1, shape[:-2] + (1, shape[-1] // 4))) * (rng.random(shape[:-2] + (1, shape[-1] // 4)) > 0.0625), 4, axis=-1).astype(np.float32)
    return mx_ref.flush(v.astype(BF))
C, K, P, R = 256, 64, 128, 3
def numbers_of(rng):
    return {"x": np.array(f(rng, N, 128, 4 * C)), "u": np.array(f(rng, N, 128, 512)), "v": np.array(f(rng, N, 128, 512))}
def mixed(rng):
    return rng.permuted(np.tile(np.arange(C), (N, 8, 1)), axis=2)
def links(e):
    return np.stack([gtable(e[r]) for r in range(N)])
def packedw(rng, w):
    c, p = packed(np.ascontiguousarray(w).reshape(N, 128, 2048), rng)
    return {"wc": c, "ws": p}
def weights(rng, still=()):
    w = np.array(f(rng, N, 128, 2048)).reshape(N, 8, 16, 4, 8, 16, 4)
    for i in still:
        w[:, :, i] = 0
        w[:, :, :, :, :, i] = 0
    return packedw(rng, w)
def setup_inputs(rng):
    return {**numbers_of(rng), "link": links(mixed(rng)), **weights(rng)}
def setup_inputs_ties(rng):
    d = numbers_of(rng)
    e = rng.permutation(N)
    x = d["x"].reshape(N, 8, 16, C, 4)
    for r in range(N):
        k = rng.permutation(C) % 3
        if r == e[0]: k = np.zeros(C, int)
        elif r in e[2::2]: k = rng.permutation(3)[np.arange(C) % 3]
        a = x[r][:, :8, :3].copy()
        a[:, :, 2] = 0
        x[r][:, :8] = a[:, :, k]
    x[e[1]] = 0
    u = d["u"].reshape(N, 8, 16, 128, 4)
    u[:, :, 8:, ::16] = 0
    u[:, :, 8:, 1::16] = 0
    t = mixed(rng)
    t[e[2]] = np.arange(C)
    t[e[3]] = t[e[3], :1].copy()
    return {"x": x.reshape(N, 128, 4 * C), "u": u.reshape(N, 128, 512), "v": d["v"], "link": links(t), **weights(rng, range(8))}
def setup_inputs_near(rng):
    d = numbers_of(rng)
    x = d["x"].astype(np.float32).reshape(N, 8, 16, C, 4)
    x[:, :, 0] = 0
    x[:, :, 8:] = 0
    u = d["u"].reshape(N, 128, 128, 4)
    u[:, :, ::16] = 0
    u[:, :, 1::16] = 0
    o = rng.permutation(N) % 4
    s = rng.integers(0, 256, (N, 8, C))
    for r in range(N):
        low = 2.0 ** -29 if o[r] == 3 else 2.0 ** -23
        for i in range(2): x[r, :, 8 + i] = ((s[r][:, :, None] >> (4 * i + np.arange(4))) & 1) * np.exp2(4.0 * i + np.arange(4)) * low
        x[r, :, 12, :, 0] = rng.integers(-1, 2, (8, C)) * (2.0 ** -29 if o[r] == 3 else 2.0 ** -20)
        if o[r] == 3: x[r, :, 13, :, 0] = x[r, :, 12, :, 0]
        if o[r] < 2:
            x[r, :, 0, :, 0] = rng.integers(0, 2, (8, C)) * 2.0 - 1.0
            x[r, :, 11, :, 0] = 2.0 ** -10
        if o[r] == 2:
            for g in range(8): x[r, g, 0, rng.permutation(C)[:2], 0] = np.array([1.0, -1.0])
        for g in rng.permutation(8)[:4]: x[r, g, 12, rng.integers(C), 0] = 2.0 ** 29 * rng.choice([-1.0, 1.0])
        k = 1.0 if o[r] == 0 else 2.0 ** -30
        for h in range(0, 128, 16):
            if o[r] < 2:
                u[r, h, h, 0] = k
                u[r, h + 11, h, 0] = k
            if o[r] == 2: u[r, h, h, 0] = 1.0
            u[r, h + 8, h] = k
            u[r, h + 9, h] = k
            u[r, h + 12, h + 1, 0] = 1.125 * 2.0 ** -30 if o[r] == 3 else 2.0 ** -30
            if o[r] == 3: u[r, h + 13, h + 1, 0] = -1.0 * 2.0 ** -30
    return {"x": x.reshape(N, 128, 4 * C).astype(BF), "u": u.reshape(N, 128, 512), "v": d["v"], "link": links(mixed(rng)), **weights(rng, [0, 8, 9, 10, 11, 12, 13, 14, 15])}
def setup_inputs_caps(rng):
    d = numbers_of(rng)
    x = np.zeros((N, 8, 16, C, 4))
    z = (N, 8, 8, C, 4)
    x[:, :, :8] = rng.choice([-1.0, 1.0], z) * (1.0 + (2 * rng.integers(0, 64, z) + 1) * 2.0 ** -7) * np.exp2(-1.0 * rng.integers(8, 15, z))
    x[:, :, 0, :, 0] = rng.choice([1.96875, 1.84375], (N, 8, C))
    s = mixed(rng)
    for i in range(3): x[:, :, 8 + i] = ((s[:, :, :, None] >> (4 * i + np.arange(4))) & 1) * np.exp2(4.0 * i + np.arange(4))
    side = rng.permutation(N) % 2 * 2 - 1
    q = np.argsort(-s * side[:, None, None], axis=2)[:, :, 1::2]
    one = rng.random((N, 8, C)) < 0.5
    a = rng.permutation(8)
    for i in range(6):
        g, t, k = a[i], i % R, 0
        for r in range(N):
            if (r >> t) & 1: one[r, g] = True
            else:
                n = K if i < 3 else K - 1 + 2 * (k % 2)
                k += 1
                one[r, g, q[r, g]] = rng.permutation(P) < n
    one[:, a[6]] = (((np.arange(N) >> (R - 1)) & 1) == 1)[:, None]
    one[:, a[7]] = ((np.arange(N) & 1) == 1)[:, None]
    x[:, :, 12, :, 0] = np.where(one, 1.0, -1.0 * rng.integers(0, 2, (N, 8, C)))
    u = d["u"].reshape(N, 128, 128, 4)
    u[:, :, ::16] = 0
    u[:, :, 1::16] = 0
    for r in range(N):
        for h in range(0, 128, 16):
            u[r, h + 8:h + 11, h] = float(side[r])
            u[r, h + 12, h + 1, 0] = 1.0
    return {"x": x.astype(np.float32).reshape(N, 128, 4 * C).astype(BF), "u": u.reshape(N, 128, 512), "v": d["v"], "link": links(mixed(rng)), **weights(rng, range(8, 16))}
def setup_inputs_huge(rng):
    d = numbers_of(rng)
    o = rng.permutation(N)
    c = rng.integers(0, 2, (N, 1, 1, C, 1)) * 2.0 - 1.0
    c[:, :, :, :2] = np.array([1.0, -1.0])[:, None]
    c[o == 1] = -1.0
    c[o == 2] = 1.0
    x = 0.6 + 0.09 * rng.random((N, 8, 16, C, 4))
    x[o == 0] = np.where(rng.random((1, 8, 16, C, 4)) < 0.125, 0.8125, 0.875)
    u = d["u"].reshape(N, 128, 128, 4)
    for i in range(2):
        a = 2.0 ** 29 * (1.0 - 0.1 * rng.random((N, 128, 8, 4)))
        a[o == 0] = 2.0 ** 30 * np.where(rng.random((1, 128, 8, 4)) < 0.03125, 0.875, 1.0)
        turned = (o % 2 == 1) if i else (o == 0) | (o > N // 2)
        for r in range(N):
            if turned[r]: a[r] *= (rng.permutation(8) % 2 * 2.0 - 1.0)[None, :, None]
        u[:, :, i::16] = a.astype(np.float32).astype(BF)
    w = np.zeros((N, 128, 4, 128, 4), np.float32)
    i = np.arange(128)
    for b in range(4): w[:, i, b, i, b] = 1
    return {"x": (2.0 ** 30 * x * c).astype(np.float32).reshape(N, 128, 4 * C).astype(BF), "u": u.reshape(N, 128, 512), "v": d["v"], "link": links(mixed(rng)), **packedw(rng, w.astype(BF))}
def setup_inputs_spread(rng):
    d = setup_inputs(rng)
    d["x"] = wide(rng, N, 128, 4 * C, cols=6)
    return d
def check_inputs(d):
    b = []
    for k in ("x", "u", "v"):
        a = np.abs(d[k].astype(np.float32))
        if not (np.isfinite(a).all() and ((a == 0) | (a >= 2.0 ** -30) & (a <= 2.0 ** 30)).all()): b.append("a value of " + k)
    none, least, most = [emit(mx_ref.quantize(np.full((128, 16), k, np.float32).astype(BF)))[1][0, 0] for k in (0.0, 2.0 ** -30, 2.0 ** 30)]
    for r in range(N):
        if (np.sort(gentries(d["link"][r]), axis=1) != np.arange(C)).any(): b.append("link: a group's entries are no permutation")
        if ((d["wc"][r] == 0x7F) | (d["wc"][r] == 0xFF)).any(): b.append("wc: a code that is no number")
        s = mx_ref.live(d["ws"][r])
        if ((s != none) & ((s < least) | (s > most))).any(): b.append("ws: a scale out of range")
    return b
def at(a, e):
    return np.take_along_axis(a, e, axis=1)
def reference(x, u, v, link, wc, ws):
    qu = [mx_ref.quantize(u[r]) for r in range(N)]
    lay = [pk(wc[r], ws[r]) for r in range(N)]
    now = [x[r] for r in range(N)]
    to = [gentries(link[r]) for r in range(N)]
    for t in range(R):
        d = 2 ** t
        own, order, bit = [], [], []
        for r in range(N):
            q = mx_ref.quantize(now[r])
            own.append(decode(q))
            s = mx_ref.matmul(qu[r], q)
            order.append(np.argsort(-(s[::16] + np.float32(0.0)), axis=1, kind="stable"))
            bit.append(s[1::16] > 0)
        kept, names, left, places, turned = [], [], [], [], []
        for r in range(N):
            k, q = order[r][:, 0::2], order[r][:, 1::2]
            there = at(to[r], q)
            fails = at(bit[r], q) != at(bit[(r + d) % N], there)
            j = np.argsort(fails.astype(np.int64), axis=1, kind="stable")
            k, q, there = at(k, j), at(q, j), at(there, j)
            h = own[r].astype(BF)
            a = ((gcols(h, k).astype(np.float32) + gcols(h, q).astype(np.float32)) * np.float32(0.5)).astype(BF)
            kept.append(mx_ref.quantize(np.ascontiguousarray(a[:, :4 * K])))
            left.append(mx_ref.quantize(np.ascontiguousarray(a[:, 4 * K:])))
            names.append(there[:, :K])
            places.append(q[:, K:])
            m = np.tile(np.arange(C), (8, 1))
            np.put_along_axis(m, k[:, K:], q[:, K:], axis=1)
            np.put_along_axis(m, q[:, K:], k[:, K:], axis=1)
            turned.append(at(to[r], m))
        to = [at(turned[(r + d) % N], to[r]) for r in range(N)]
        for r in range(N):
            c = (r - d) % N
            slots = join(kept[c], left[r])
            e = np.full((8, C), P)
            np.put_along_axis(e, places[r], np.tile(np.arange(K, P), (8, 1)), axis=1)
            np.put_along_axis(e, names[c], np.tile(np.arange(K), (8, 1)), axis=1)
            made = []
            for b in range(4):
                h = mx_ref.matmul(pick(lay[r], np.arange(128 * b, 128 * b + 128)), slots)
                h = np.concatenate([h, np.zeros((128, 1), np.float32)], axis=1)
                made.append(gpick(h, e) * np.float32(0.03125) + own[r][:, b::4])
            now[r] = tile(made)
    y, lk = np.zeros((N, 128, C), np.float32), np.zeros((N, 8, C), np.float32)
    oc, osc = np.zeros((N, 128, 4 * C), np.uint8), np.zeros((N, 16, C), np.uint8)
    for r in range(N):
        q = mx_ref.quantize(now[r])
        y[r] = mx_ref.matmul(mx_ref.quantize(v[r]), q)
        lk[r] = to[r]
        oc[r], osc[r] = emit(q)
    return {"y": y, "lk": lk, "oc": oc, "osc": osc}

import numpy as np
from concourse.mybir import dt, AluOpType, ActivationFunctionType

R = 3
LATE = 9

SCRATCH = {
    "x0": ("sbuf", [128, 1024], "bfloat16"),
    "xc": ("sbuf", [128, 1024], "bfloat16"),
    "qx": ("sbuf", [128, 256], "float8_e4m3fn_x4"),
    "sx": ("sbuf", [128, 256], "uint8"),
    "ub": ("sbuf", [128, 512], "bfloat16"),
    "vb": ("sbuf", [128, 512], "bfloat16"),
    "wq": ("sbuf", [128, 512], "float8_e4m3fn_x4"),
    "wp": ("sbuf", [128, 512], "uint8"),
    "qu": ("sbuf", [128, 128], "float8_e4m3fn_x4"),
    "su": ("sbuf", [128, 128], "uint8"),
    "qur": ("sbuf", [128, 256], "float8_e4m3fn_x4"),
    "sur": ("sbuf", [128, 256], "uint8"),
    "qv": ("sbuf", [128, 128], "float8_e4m3fn_x4"),
    "sv": ("sbuf", [128, 128], "uint8"),
    "ec": ("sbuf", [128, 2048], "bfloat16"),
    "qe": ("sbuf", [128, 512], "float8_e4m3fn_x4"),
    "se": ("sbuf", [128, 512], "uint8"),
    "unit": ("sbuf", [128, 128], "bfloat16"),
    "oi": ("sbuf", [128, 128], "int32"),
    "oj": ("sbuf", [128, 128], "int32"),
    "ob": ("sbuf", [128, 128], "bfloat16"),
    "oc4": ("sbuf", [128, 512], "bfloat16"),
    "qo": ("sbuf", [128, 128], "float8_e4m3fn_x4"),
    "so": ("sbuf", [128, 128], "uint8"),
    "ji": ("sbuf", [128, 256], "int32"),
    "jm": ("sbuf", [128, 256], "int32"),
    "dm": ("sbuf", [128, 256], "bfloat16"),
    "dm2": ("sbuf", [128, 128], "bfloat16"),
    "nd": ("sbuf", [128, 256], "bfloat16"),
    "ib": ("sbuf", [128, 256], "bfloat16"),
    "i1": ("sbuf", [128, 256], "bfloat16"),
    "pat": ("sbuf", [128, 256], "bfloat16"),
    "pmw": ("sbuf", [128, 16], "bfloat16"),
    "sg": ("sbuf", [128, 256], "bfloat16"),
    "bm": ("sbuf", [128, 256], "bfloat16"),
    "bh": ("sbuf", [128, 256], "bfloat16"),
    "m1": ("sbuf", [128, 256], "float32"),
    "st": ("sbuf", [128, 256], "float32"),
    "cl": ("sbuf", [128, 1024], "bfloat16"),
    "ct": ("sbuf", [128, 2048], "bfloat16"),
    "cj": ("sbuf", [128, 4096], "bfloat16"),
    "qc": ("sbuf", [128, 256], "float8_e4m3fn_x4"),
    "sc": ("sbuf", [128, 256], "uint8"),
    "cm": ("sbuf", [128, 128], "bfloat16"),
    "ch": ("sbuf", [128, 128], "bfloat16"),
    "eqb": ("sbuf", [128, 256], "bfloat16"),
    "kk": ("sbuf", [128, 256], "bfloat16"),
    "tw": ("sbuf", [128, 512], "bfloat16"),
    "zd": ("sbuf", [128, 256], "float32"),
    "zw": ("sbuf", [128, 256], "float32"),
    "za": ("sbuf", [128, 256], "float32"),
    "fl": ("sbuf", [128, 128], "bfloat16"),
    "fm": ("sbuf", [128, 128], "bfloat16"),
    "ft": ("sbuf", [128, 128], "bfloat16"),
    "uu": ("sbuf", [128, 128], "bfloat16"),
    "um": ("sbuf", [128, 128], "bfloat16"),
    "uh": ("sbuf", [128, 128], "bfloat16"),
    "pk": ("sbuf", [128, 256], "float32"),
    "pw": ("sbuf", [128, 128], "float32"),
    "pq": ("sbuf", [128, 128], "float32"),
    "ph": ("sbuf", [128, 128], "float32"),
    "at": ("sbuf", [128, 512], "bfloat16"),
    "lp": ("sbuf", [128, 256], "bfloat16"),
    "nm": ("sbuf", [128, 64], "bfloat16"),
    "nn": ("sbuf", [128, 64], "bfloat16"),
    "nh": ("sbuf", [128, 64], "bfloat16"),
    "em": ("sbuf", [128, 256], "bfloat16"),
    "eh": ("sbuf", [128, 256], "bfloat16"),
    "lr": ("sbuf", [128, 256], "bfloat16"),
    "lvl": ("sbuf", [128, 128], "bfloat16"),
    "tb": ("sbuf", [128, 256], "bfloat16"),
    "tm": ("sbuf", [128, 256], "bfloat16"),
    "th": ("sbuf", [128, 256], "bfloat16"),
    "tr": ("sbuf", [128, 256], "bfloat16"),
    "lm": ("sbuf", [128, 256], "bfloat16"),
    "lh": ("sbuf", [128, 256], "bfloat16"),
    "lkf": ("sbuf", [128, 256], "float32"),
    "ys": ("sbuf", [128, 256], "float32"),
    "pb": ("psum", [128, 512], "float32"),
    "ps": ("psum", [128, 512], "float32"),
    "pg0": ("psum", [128, 512], "float32"),
    "pg1": ("psum", [128, 512], "float32"),
}
for _b in range(4):
    SCRATCH["fh%d" % _b] = ("sbuf", [128, 256], "bfloat16")
    SCRATCH["gk%d" % _b] = ("sbuf", [128, 128], "bfloat16")
    SCRATCH["hs%d" % _b] = ("sbuf", [128, 136], "float32")
    SCRATCH["pf%d" % _b] = ("psum", [128, 512], "float32")
    if _b < 2:
        SCRATCH["fs%d" % _b] = ("sbuf", [128, 256], "bfloat16")
    else:
        SCRATCH["hg%d" % _b] = ("sbuf", [128, 256], "float32")
for _t in range(R):
    SCRATCH["ew%d" % _t] = ("sbuf", [128, 256], "bfloat16")
    SCRATCH["vk%d" % _t] = ("sbuf", [128, 128], "float8_e4m3fn_x4")
    SCRATCH["vt%d" % _t] = ("sbuf", [128, 128], "uint8")
    SCRATCH["vq%d" % _t] = ("sbuf", [128, 192], "float8_e4m3fn_x4")
    SCRATCH["vs%d" % _t] = ("sbuf", [128, 192], "uint8")

PART = {}


def share(buf, dtype, names):
    for k, (name, n) in enumerate(names):
        PART[name] = (buf, 16 * k, n)
    SCRATCH[buf] = ("sbuf", [128, 16 * len(names)], dtype)


share("wi", "int32", [("uli", 16), ("ja", 8), ("jb", 8), ("jr", 8), ("pi", 8), ("qi", 8)])
share("wl", "int32", [("li", 16)])
share("wf", "float32", [("nb", 16), ("lof", 16), ("ck", 8), ("rs", 16), ("rtf", 16), ("jc", 8), ("j2", 8), ("p1", 8), ("jp", 8),
                        ("cf", 8), ("jh", 8), ("mf", 8), ("nf", 8)])
share("wo", "uint16", [("ul", 16), ("lo", 16), ("rt", 16), ("nu", 8), ("nt", 4), ("et", 16)])
share("ws1", "uint16", [(_n + str(_t), 16) for _t in range(R) for _n in ("bt", "kq", "tt", "lt")])
share("wa", "uint16", [(_n + str(_t), _k) for _t in range(R) for _n, _k in (("ab", 16), ("aq", 4), ("an", 16), ("al", 16))])

SEMAPHORES = ["cv", "ca", "ct", "cp", "ls", "st", "lx", "lu", "lv", "ll", "lwc", "lws"]
for _t in range(R):
    SEMAPHORES += [_n + str(_t) for _n in ("rb", "rq", "rc", "rn", "rt", "rl")]


def overlap(a, b):
    if a[0] != b[0] or a[1] >= b[2] or b[1] >= a[2]:
        return False
    if a[3] == b[3] and a[3] > 1 and (a[1] - b[1]) % a[3]:
        return False
    return True


def rank_program(g, core, T, topo):
    rank = T.rank_of(core)
    if rank is None:
        return
    N = len(T.cores)
    A = AluOpType
    F = ActivationFunctionType
    queues = {"v": g.vector, "a": g.scalar, "t": g.tensor, "g": g, "s": g.sync}
    csem = {"v": "cv", "a": "ca", "t": "ct", "g": "cp"}
    known = {k: {} for k in queues}
    total = {}
    log = {}

    def merge(dst, src):
        for k, n in src.items():
            if dst.get(k, 0) < n:
                dst[k] = n

    def order(q, rd, wr):
        need = []
        for acc, w in [(r, False) for r in rd] + [(r, True) for r in wr]:
            ps = SCRATCH[acc[0]][0] == "psum"
            for (eq, sem, val, reg, ew, clk) in log.get(acc[0], []):
                if not (w or ew or (ps and eq != q)):
                    continue
                if not ps and not overlap(acc, reg):
                    continue
                if known[q].get(sem, 0) < val:
                    need.append((sem, val, clk))
        best = {}
        for sem, val, clk in need:
            if sem not in best or best[sem][0] < val:
                best[sem] = (val, clk)
        for sem in list(best):
            val, clk = best[sem]
            if any(o != sem and best[o][1].get(sem, 0) >= val for o in best):
                continue
            queues[q].wait_ge(T.sem[sem], val)
        for sem, (val, clk) in best.items():
            merge(known[q], clk)
            merge(known[q], {sem: val})

    def note(q, sem, val, rd, wr):
        clk = dict(known.get(q, {}))
        merge(clk, {sem: val})
        for acc, w in [(r, False) for r in rd] + [(r, True) for r in wr]:
            log.setdefault(acc[0], []).append((q, sem, val, acc, w, clk))

    def op(q, fn, rd, wr, sem=None, inc=1):
        order(q, rd, wr)
        sem = sem or csem[q]
        total[sem] = total.get(sem, 0) + inc
        fn().then_inc(T.sem[sem], inc)
        note(q, sem, total[sem], rd, wr)

    def reg(name, lo=0, hi=None, step=1):
        if name in PART:
            buf, base, n = PART[name]
            return (buf, base + lo, base + (n if hi is None else hi), step)
        return (name, lo, SCRATCH[name][1][1] if hi is None else hi, step)

    def ap(r):
        if r[3] == 1:
            return T[r[0]][:, r[1]:r[2]]
        return T[r[0]][:, r[1]:r[2]:r[3]]

    def load(q, r, src, sem, codes=False):
        o = ap(r)
        if codes:
            o = o.bitcast(dt.uint8)
        op(q, lambda: queues[q].dma_start(o, src), [], [r], sem, 16)

    def ts(o, i, s1, op0, s2=None, op1=None):
        rd = [i]
        a1, a2 = s1, s2
        if isinstance(s1, tuple):
            rd.append(s1)
            a1 = ap(s1)
        if isinstance(s2, tuple):
            rd.append(s2)
            a2 = ap(s2)
        if op1 is None:
            op("v", lambda: g.vector.tensor_scalar(ap(o), ap(i), a1, None, op0), rd, [o])
        else:
            op("v", lambda: g.vector.tensor_scalar(ap(o), ap(i), a1, a2, op0, op1), rd, [o])

    def tt(o, i0, i1, f, off=None):
        rd = [i0, i1]
        a0 = ap(i0)
        if off is not None:
            rd.append(off)
            a0 = a0.indirect(ap(off))
        op("v", lambda: g.vector.tensor_tensor(ap(o), a0, ap(i1), f), rd, [o])

    def copy(o, i, off=None, scatter=None):
        rd = [i]
        ai, ao = ap(i), ap(o)
        if off is not None:
            rd.append(off)
            ai = ai.indirect(ap(off))
        if scatter is not None:
            rd.append(scatter)
            ao = ao.indirect(ap(scatter))
        op("v", lambda: g.vector.tensor_copy(ao, ai), rd, [o])

    def fill(o, c):
        op("v", lambda: g.vector.memset(ap(o), c), [], [o])

    def scan(o, d0, d1, f0, f1):
        op("v", lambda: g.vector.tensor_tensor_scan(ap(o), ap(d0), ap(d1), 0.0, f0, f1), [d0, d1], [o])

    def act(o, i, f, scale=None, bias=None, off=None, acc=None):
        rd, wr, kw = [i], [o], {}
        ai = ap(i)
        if off is not None:
            rd.append(off)
            ai = ai.indirect(ap(off))
        if scale is not None:
            kw["scale"] = scale
        if bias is not None:
            kw["bias"] = bias
        if acc is not None:
            kw["accum_out"] = ap(acc)
            wr.append(acc)
        op("a", lambda: g.scalar.activation(ap(o), ai, f, **kw), rd, wr)

    def quant(qo, so, i):
        op("v", lambda: g.vector.quantize_mx(ap(qo), ap(so), ap(i)), [i], [qo, so])

    def mm(o, wq, wsc, xq, xs, start=True, stop=True):
        op("t", lambda: g.tensor.matmul_mx(ap(o), ap(wq), ap(wsc), ap(xq), ap(xs), start, stop), [wq, wsc, xq, xs], [o])

    def iota(o, pattern, base, cm, flag=False):
        if flag:
            op("g", lambda: g.iota(ap(o), pattern, base, cm, allow_small_or_imprecise_dtypes=True), [], [o])
        else:
            op("g", lambda: g.iota(ap(o), pattern, base, cm), [], [o])

    def send(to, r_src, r_dst, sem, codes=False):
        dst = T.cores[to % N]
        order("g", [r_src], [])
        rid, pid = topo.addr(dst, core)
        o, i = ap(r_dst), ap(r_src)
        if codes:
            o, i = o.bitcast(dt.uint8), i.bitcast(dt.uint8)
        g.remote_dma(o, i, T.sem[sem], T.sem["ls"], pid, rid, topo.mask(core, dst))
        total["ls"] = total.get("ls", 0) + len(topo.engines(core, dst))

    def arrive(frm, regs, sem):
        total[sem] = len(topo.engines(T.cores[frm % N], core))
        note("", sem, total[sem], [], regs)

    def diag(o, i, n=256, mask="dm"):
        scan(o, i, reg(mask, 0, n), A.add, A.mult)

    def hold(o, i, n=256):
        scan(o, reg("nd", 0, n), i, A.mult, A.add)

    def tab(name, n=256, lo=0):
        return reg(name, lo + 15, n, 16)

    load("s", reg("x0"), T.x[:, :], "lx")
    load("a", reg("ub"), T.u[:, :], "lu")
    load("a", reg("li"), T.link[:, :], "ll")
    load("s", reg("wq"), T.wc[:, :], "lwc", True)
    load("a", reg("wp"), T.ws[:, :], "lws")
    load("s", reg("vb"), T.v[:, :], "lv")
    iota(reg("uli"), [[1, 2], [16, 8]], 0, 0)
    iota(reg("ji"), [[1, 256]], 128, -1)
    iota(reg("oi"), [[16, 8], [0, 16]], 15, -1)
    iota(reg("ib"), [[1, 256]], 0, 0, True)
    iota(reg("i1"), [[1, 256]], 1, 0, True)
    iota(reg("pat"), [[0, 128], [512, 2]], 0, 0, True)
    iota(reg("ja"), [[0, 8]], 0, 1)
    iota(reg("jb"), [[16, 8]], 0, 0)
    fill(reg("ec"), 0.0)
    copy(reg("ul"), reg("uli"))
    ts(reg("unit"), reg("ji", 0, 128), 128.0, A.is_equal)
    ts(reg("jm"), reg("ji"), 15, A.bitwise_and)
    fill(reg("pmw"), 1.0)
    ts(reg("dm"), reg("jm"), 0.0, A.is_equal)
    fill(reg("pmw", 0, 1), -1.0)
    fill(reg("at"), 0.0)
    for b in range(4):
        act(("ec", 512 * b + b, 512 * (b + 1), 4), reg("unit"), F.Copy)
    act(reg("nd"), reg("dm"), F.Identity, scale=-1.0, bias=1.0)
    act(reg("dm2"), reg("dm", 0, 128), F.Copy, scale=2.0)
    quant(reg("qu"), reg("su"), reg("ub"))
    op("a", lambda: g.scalar.activation(T.sur[:, 0:256], T.su[:, 0:128].indirect(ap(reg("ul"))), F.Copy),
       [reg("su"), reg("ul")], [reg("sur")])

    for t in range(R):
        d = 2 ** t
        s = str(t)
        vq, vs, vk, vt = "vq" + s, "vs" + s, "vk" + s, "vt" + s
        kq, lt = "kq" + s, reg("lt" + s)
        kk_, kl, qk, ql = reg(kq, 0, 4), reg(kq, 4, 8), reg(kq, 8, 12), reg(kq, 12, 16)
        arrive(rank + d, [reg("ab" + s)], "rb" + s)
        arrive(rank - d, [reg("aq" + s)], "rq" + s)
        arrive(rank - d, [(vq, 128, 192, 1)], "rc" + s)
        arrive(rank - d, [(vs, 128, 192, 1)], "rn" + s)
        arrive(rank + d, [reg("an" + s)], "rt" + s)
        arrive(rank - d, [reg("al" + s)], "rl" + s)
        quant(reg("qx"), reg("sx"), reg("xc" if t else "x0"))
        if t == 0:
            op("v", lambda: g.vector.tensor_copy(T.qur[:, 0:256].bitcast(dt.uint32),
                                                 T.qu[:, 0:128].bitcast(dt.uint32).indirect(ap(reg("ul")))),
               [reg("qu"), reg("ul")], [reg("qur")])
        X = (reg("qx"), reg("sx"))
        mm(reg("pb", 0, 256), reg("qur", 128, 256), reg("sur", 128, 256), *X)
        mm(reg("ps", 0, 256), reg("qur", 0, 128), reg("sur", 0, 128), *X)
        act(reg("sg"), reg("pb", 0, 256), F.Sign)
        if t:
            diag(reg("lm"), reg("lr"))
            hold(reg("lh"), reg("lm"))
            copy(lt, tab("lh"))
        else:
            copy(lt, reg("li"))
            quant(reg("qe"), reg("se"), reg("ec"))
        send(rank + d, lt, reg("al" + s), "rl" + s)
        for b in range(4):
            mm(reg("pf%d" % b, 0, 256), reg("qe", 128 * b, 128 * b + 128), reg("se", 128 * b, 128 * b + 128), *X)
        tt(reg("m1"), reg("ps", 0, 256), reg("dm"), A.mult)
        diag(reg("bm"), reg("sg"))
        hold(reg("st"), reg("m1"))
        hold(reg("bh"), reg("bm"))

        def compare(m):
            own = ("st", 16 * m + 15, 16 * m + 16, 1)
            e = 16 * m + 16
            n = 256 if m >= 8 else 128
            a = 1024 * ((m - 8) // 4)

            def blk(lo, hi):
                if m >= 8:
                    return ("ct", a + m % 4 + 4 * lo, a + 4 * hi, 4)
                return ("cl", 128 * m + lo, 128 * m + hi, 1)
            ts(blk(0, e), reg("ps", 0, e), own, A.is_ge)
            if e < n:
                ts(blk(e, n), reg("ps", e, n), own, A.is_gt)
            act(("cj", 256 * m, 256 * m + n, 1), blk(0, n), F.Copy, acc=reg("rs", m, m + 1))

        for k, m in enumerate(list(range(8, 16)) + list(range(8))):
            compare(m)
            if k == 0:
                ts(reg("bt" + s), tab("bh"), 0.0, A.is_gt)
                send(rank - d, reg("bt" + s), reg("ab" + s), "rb" + s)
                ts(reg("nb"), tab("bh"), 0.0, A.is_le, 256.0, A.mult)
            if k == 1:
                tt(reg("lof"), reg("nb"), tab("lh") if t else reg("li"), A.add)
                if t == 0:
                    ts(reg("oj"), reg("oi"), 4, A.arith_shift_right)
            if k == 2:
                copy(reg("lo"), reg("lof"))
                if t == 0:
                    ts(reg("ob"), reg("oj"), 0.0, A.is_equal)
                    for b in range(4):
                        act(("oc4", b, 512, 4), reg("ob"), F.Copy)
            if k == 5:
                quant(reg("qc", 0, 128), reg("sc", 0, 128), reg("ct", 0, 512))
                if t == 0:
                    quant(reg("qo"), reg("so"), reg("oc4"))
            if k == 8:
                quant(reg("qc", 128, 256), reg("sc", 128, 256), reg("ct", 1024, 1536))
                mm(reg("pb", 0, 128), reg("qo"), reg("so"), reg("qc", 0, 128), reg("sc", 0, 128), True, False)
                mm(reg("pb", 0, 128), reg("qo"), reg("so"), reg("qc", 128, 256), reg("sc", 128, 256), False, True)
                tt(reg("eqb"), reg("ps", 0, 256), reg("st"), A.is_equal)
            if k == 9:
                hold(reg("kk"), reg("eqb"))
            if k == 11:
                diag(reg("cm"), reg("pb", 0, 128), 128)
            if k == 12:
                hold(reg("ch"), reg("cm"), 128)
            if k == 13:
                tt(reg("ck"), tab("ch", 128), tab("kk", 128), A.add)
            if k == 14:
                tt(reg("rtf", 8, 16), reg("rs", 8, 16), tab("kk", 256, 128), A.subtract)
            if k == LATE:
                act(reg("tw", 0, 256), reg("pmw"), F.Copy, off=reg("ab" + s))
                act(reg("tw", 256, 512), reg("tw", 0, 256), F.Copy, scale=-1.0)
        copy(reg("rt", 8, 16), reg("rtf", 8, 16))
        tt(reg("zd"), reg("tw"), reg("i1"), A.mult, off=reg("lo"))
        tt(reg("rtf", 0, 8), reg("rs", 0, 8), reg("ck"), A.subtract)
        ts(reg("rt", 0, 8), reg("rtf", 0, 8), 128.0, A.add)
        for b in range(4):
            act(reg("fh%d" % b), reg("pf%d" % b, 0, 256), F.Copy, scale=0.5)
        if t == 0:
            ts(reg("jr"), reg("ja"), 15, A.bitwise_and)
            act(reg("lr"), reg("ib"), F.Copy, off=reg("lt0"))
        copy(reg("zw"), reg("zd"), scatter=reg("rt"))
        act(reg("za"), reg("zw"), F.Abs)
        act(reg("lp"), reg("ib"), F.Copy, off=reg("al" + s))
        act(reg("tb"), reg("lr"), F.Copy)
        if t == 0:
            for b in range(4):
                act(reg("hs%d" % b, 128, 136), reg("ib", 0, 8), F.Copy, scale=0.0)
            for i in range(R):
                act(reg("ew%d" % i), reg("ib"), F.Identity, scale=0.0, bias=128.0)
            tt(reg("jc"), reg("jr"), reg("jb"), A.add)
        ts(reg("fl"), reg("zw", 1, 256, 2), 0.0, A.is_lt)
        if t == 0:
            ts(reg("j2"), reg("jc"), 2.0, A.mult)
        scan(reg("uu"), reg("fl"), reg("fl"), A.add, A.add)
        diag(reg("fm"), reg("fl"), 128, "dm2")
        ts(reg("p1", 0, 1), reg("uu", 127, 128), -0.5, A.mult, 127.0, A.add)
        diag(reg("um"), reg("uu"), 128)
        hold(reg("ft"), reg("fm"), 128)
        ts(reg("jp"), reg("jc"), -1.0, A.mult, reg("p1", 0, 1), A.add)
        hold(reg("uh"), reg("um"), 128)
        scan(reg("pk", 0, 128), reg("pat", 0, 128), reg("za", 0, 128), A.mult, A.add)
        tt(reg("cf"), tab("uh", 128), reg("jp"), A.add)
        tt(reg("jh"), reg("j2"), tab("uh", 128), A.subtract)
        tt(reg("mf"), reg("cf"), tab("ft", 128), A.mult)
        scan(reg("pk", 128, 256), reg("pat", 128, 256), reg("za", 128, 256), A.mult, A.add)
        tt(reg("nf"), reg("jh"), reg("mf"), A.add)
        ts(reg("nu"), reg("nf"), 0.5, A.mult)
        copy(reg("pw"), reg("pk", 1, 256, 2), scatter=reg("nu"))
        diag(reg("pq"), reg("pw"), 128)
        hold(reg("ph"), reg("pq"), 128)
        ts(reg(kq, 0, 8), tab("ph", 128), 1.0 / 512, A.mult, -1.0 - 1.0 / 1024, A.add)
        copy(reg("pi"), tab("ph", 128))
        copy(reg("gk0", 0, 64), reg("fh0"), off=kk_)
        for b in range(1, 4):
            act(reg("gk%d" % b, 0, 64), reg("fh%d" % b), F.Copy, off=kk_)
        ts(reg("qi"), reg("pi"), 511, A.bitwise_and)
        ts(reg(kq, 8, 16), reg("qi"), -1.0, A.add)
        send(rank + d, qk, reg("aq" + s), "rq" + s)
        for b in range(4):
            tt(("at", b, 256, 4), reg("fh%d" % b), reg("gk%d" % b, 0, 64), A.add, off=qk)
        quant(reg(vk), reg(vt), reg("at"))
        send(rank + d, (vk, 0, 64, 1), (vq, 128, 192, 1), "rc" + s, True)
        send(rank + d, (vt, 0, 64, 1), (vs, 128, 192, 1), "rn" + s)
        act(reg("lvl", 0, 64), reg("lr"), F.Copy, off=ql)
        act(reg("lvl", 64, 128), reg("lr"), F.Copy, off=kl)
        for b in range(4):
            act(reg("gk%d" % b, 64, 128), reg("fh%d" % b), F.Copy, off=kl)

        def left(b):
            tt(("at", 256 + b, 512, 4), reg("fh%d" % b), reg("gk%d" % b, 64, 128), A.add, off=ql)
        ew = reg("ew" + s)
        copy(ew, reg("ib", 0, 64), scatter=ql)
        copy(reg("tb"), reg("lvl", 0, 64), scatter=kl)
        copy(reg("tb"), reg("lvl", 64, 128), scatter=ql)
        left(0)
        diag(reg("tm"), reg("tb"))
        left(1)
        hold(reg("th"), reg("tm"))
        left(2)
        copy(reg("tt" + s), tab("th"))
        left(3)
        send(rank - d, reg("tt" + s), reg("an" + s), "rt" + s)
        act(reg("nm"), reg("lp"), F.Copy, off=reg("aq" + s))
        for b in range(2):
            act(reg("fs%d" % b), reg("fh%d" % b), F.Copy, scale=2.0)
        diag(reg("nn"), reg("nm"), 64)
        quant((vq, 0, 128, 1), (vs, 0, 128, 1), reg("at"))
        hold(reg("nh"), reg("nn"), 64)
        if t == 0:
            quant(reg("qv"), reg("sv"), reg("vb"))
        copy(reg("nt"), tab("nh", 64))
        copy(ew, reg("ib", 64, 128), scatter=reg("nt"))
        diag(reg("em"), ew)
        hold(reg("eh"), reg("em"))
        copy(reg("et"), tab("eh"))
        ph = ["pg0", "pg1", "pb", "ps"]
        for b in (2, 0, 1, 3):
            mm(reg(ph[b], 0, 128), reg("wq", 128 * b, 128 * b + 128), reg("wp", 128 * b, 128 * b + 128),
               (vq, 64, 192, 1), (vs, 64, 192, 1))
        for b in (2, 3):
            act(reg("hs%d" % b, 0, 128), reg(ph[b], 0, 128), F.Copy, scale=0.03125)
            act(reg("hg%d" % b), reg("hs%d" % b, 0, 129), F.Copy, off=reg("et"))
        for b in (0, 1):
            ts(reg("hs%d" % b, 0, 128), reg(ph[b], 0, 128), 0.03125, A.mult)
        for b in (0, 1):
            tt(reg("xc", b, 1024, 4), reg("hs%d" % b, 0, 129), reg("fs%d" % b), A.add, off=reg("et"))
        for b in (2, 3):
            tt(reg("xc", b, 1024, 4), reg("hg%d" % b), reg("pf%d" % b, 0, 256), A.add)
        act(reg("tr"), reg("ib"), F.Copy, off=reg("an" + s))
        act(reg("lkf" if t == R - 1 else "lr"), reg("tr"), F.Copy, off=lt)

    quant(reg("qx"), reg("sx"), reg("xc"))
    mm(reg("ps", 0, 256), reg("qv"), reg("sv"), reg("qx"), reg("sx"))
    op("s", lambda: g.sync.dma_start(T.oc[:, :], T.qx[:, 0:256].bitcast(dt.uint8)), [reg("qx")], [], "st", 16)
    copy(reg("ys"), reg("ps", 0, 256))
    op("s", lambda: g.sync.dma_start(T.y[:, :], T.ys[:, :]), [reg("ys")], [], "st", 16)
    for k in range(4):
        op("s", lambda: g.sync.dma_start(T.osc[4 * k:4 * k + 4, 0:256], T.sx[32 * k:32 * k + 4, 0:256]), [reg("sx")], [], "st", 16)
    op("s", lambda: g.sync.dma_start(T.lk[:, :], T.lkf[0:128:16, :]), [reg("lkf")], [], "st", 16)
    for sem in SEMAPHORES:
        if total.get(sem, 0):
            g.wait_ge(T.sem[sem], total[sem])
